import numpy as np
import ml_dtypes


def mxq(x, axis, fmt="e4m3"):
    dtype, down = {"e4m3": (ml_dtypes.float8_e4m3fn, 7), "e5m2": (ml_dtypes.float8_e5m2, 14)}[fmt]
    v = np.moveaxis(np.asarray(x, np.float32).astype(ml_dtypes.bfloat16).astype(np.float64), axis, -1)
    blocks = v.reshape(v.shape[:-1] + (-1, 32))
    amax = np.abs(blocks).max(-1, keepdims=True)
    byte = np.maximum(np.where(amax > 0, np.frexp(amax)[1] - 1 + 127, 0) - down, 1)
    scale = np.exp2(byte - 127.0)
    codes = (blocks / scale).astype(np.float32).astype(dtype).astype(np.float64)
    return np.moveaxis((codes * scale).reshape(v.shape), -1, axis)


WIDE = False


def mx_kscale(k):
    if not WIDE:
        return np.ones(k)
    levels = np.array([30, -30])
    if k % 512:
        return np.exp2(np.random.permutation(np.resize(levels, k // 32))).repeat(32)
    a = np.empty((k // 512, 16))
    for p in range(k // 512):
        a[p, :8] = np.random.permutation(np.resize(levels, 8))
        for g in range(8):
            far = levels[np.abs(levels - a[p, g]) >= 10]
            a[p, g + 8] = far[np.random.randint(len(far))]
    return np.exp2(a.ravel()).repeat(32)


def f64(x):
    return np.asarray(x).astype(np.float64)


def striped(idx):
    return np.tile(np.asarray(idx).reshape(-1, 16).T, (8, 1)).astype(np.uint16)


def unstriped(offs):
    return offs[:16].T.reshape(-1).astype(np.int64)


E2M1 = np.array([0.0, 0.5, 1.0, 1.5, 2.0, 3.0, 4.0, 6.0, -0.0, -0.5, -1.0, -1.5, -2.0, -3.0, -4.0, -6.0])


def pack_weight(w, fmt):
    k, n = w.shape
    w = f64(np.asarray(w, np.float32).astype(ml_dtypes.bfloat16)).reshape(k // 32, 32, n)
    amax = np.abs(w).max(1)
    if fmt in ("e4m3", "e5m2"):
        byte = np.frexp(amax)[1] - 1 + 127 - (7 if fmt == "e4m3" else 14)
    else:
        mant, ex = np.frexp(amax / 6.0)
        byte = np.where(mant > 0.5, ex, ex - 1) + 127
    byte = np.clip(np.where(amax > 0, byte, 1), 1, 254)
    scaled = (w * np.exp2(127.0 - byte)[:, None, :]).reshape(k, n).astype(np.float32)
    by_word = np.ascontiguousarray(scaled.reshape(k // 512, 128, 4, n).transpose(0, 1, 3, 2))
    if fmt in ("e4m3", "e5m2"):
        words = by_word.astype(ml_dtypes.float8_e4m3fn if fmt == "e4m3" else ml_dtypes.float8_e5m2).view(np.uint8)
    else:
        c = by_word.astype(ml_dtypes.float4_e2m1fn).view(np.uint8) & 0xF
        words = (c[..., 0::2] | (c[..., 1::2] << 4)).reshape(k // 512, 128, 2 * n)
    return np.ascontiguousarray(words), np.ascontiguousarray(byte.astype(np.uint8).reshape(k // 512, 16, n))


def unpack_weight(words, scales, fmt):
    g, _, n = scales.shape
    words = np.ascontiguousarray(words).reshape(g, 128, n, -1)
    if fmt in ("e4m3", "e5m2"):
        vals = words.view(ml_dtypes.float8_e4m3fn if fmt == "e4m3" else ml_dtypes.float8_e5m2).astype(np.float64)
    else:
        nib = np.empty((g, 128, n, 4), np.uint8)
        nib[..., 0::2] = words & 0xF
        nib[..., 1::2] = words >> 4
        vals = E2M1[nib]
    vals = vals * np.repeat(np.exp2(scales.astype(np.float64) - 127.0), 8, axis=1)[..., None]
    return vals.transpose(0, 1, 3, 2).reshape(g * 512, n)


K, T, Z, J, R, N, L, E = 512, 1024, 1024, 256, 512, 256, 512, 128


def setup_inputs():
    n = np.random.standard_normal
    idx = np.random.permutation(T)[:J]
    idx2 = np.random.permutation(Z)[:J]
    idx3 = np.random.permutation(J)[:E]
    idx4 = np.random.permutation(J)[:E]
    fk = mx_kscale(K)
    fr = mx_kscale(R)
    fl = mx_kscale(L)
    xtp = pack_weight(n((K, T)) / fk[:, None], "e5m2")
    xop = pack_weight(n((K, Z)) / fk[:, None], "e4m3")
    wp = pack_weight(n((K, R)) * 1 / np.sqrt(K) * fk[:, None] * fr, "e2m1")
    wbp = pack_weight(n((R, N)) * 1 / np.sqrt(R) / fr[:, None], "e2m1")
    sxp = pack_weight(n((L, J)) / fl[:, None], "e4m3")
    wsp = pack_weight(n((L, N)) * 1 / np.sqrt(L) * fl[:, None], "e2m1")
    return {
        "xt_words": xtp[0],
        "xt_scales": xtp[1],
        "xo_words": xop[0],
        "xo_scales": xop[1],
        "w_words": wp[0],
        "w_scales": wp[1],
        "wb_words": wbp[0],
        "wb_scales": wbp[1],
        "sx_words": sxp[0],
        "sx_scales": sxp[1],
        "ws_words": wsp[0],
        "ws_scales": wsp[1],
        "offs": striped(idx),
        "offs2": striped(idx2),
        "offs3": striped(idx3),
        "offs4": striped(idx4),
    }


def reference(xt_words, xt_scales, xo_words, xo_scales, w_words, w_scales, wb_words, wb_scales, sx_words, sx_scales, ws_words, ws_scales, offs, offs2, offs3, offs4):
    idx = unstriped(offs)
    idx2 = unstriped(offs2)
    idx3 = unstriped(offs3)
    idx4 = unstriped(offs4)
    xtu = unpack_weight(xt_words, xt_scales, "e5m2")
    xou = unpack_weight(xo_words, xo_scales, "e4m3")
    wu = unpack_weight(w_words, w_scales, "e2m1")
    wbu = unpack_weight(wb_words, wb_scales, "e2m1")
    sxu = unpack_weight(sx_words, sx_scales, "e4m3")
    wsu = unpack_weight(ws_words, ws_scales, "e2m1")
    xtidxg = xtu[:, idx]
    a = wu.T @ xtidxg
    xoidx2g = xou[:, idx2]
    b = wu.T @ xoidx2g
    hid = np.maximum(a, b)
    hidq = mxq(hid, 0, "e4m3")
    p = wbu.T @ hidq + wsu.T @ sxu
    y = np.maximum(p[:, idx3], p[:, idx4])
    return y

@@ -1,0 +1,193 @@
+from contextlib import ExitStack
+
+import concourse.mybir as mybir
+
+K, T, Z, J, R, N, L, E = 512, 1024, 1024, 256, 512, 256, 512, 128
+FLOPS = 2 * (2 * K * R * J + R * N * J + L * N * J)
+
+F32 = mybir.dt.float32
+BF16 = mybir.dt.bfloat16
+I32 = mybir.dt.int32
+U32 = mybir.dt.uint32
+U16 = mybir.dt.uint16
+U8 = mybir.dt.uint8
+E4M3 = mybir.dt.float8_e4m3fn_x4
+E5M2 = mybir.dt.float8_e5m2_x4
+E2M1 = mybir.dt.float4_e2m1fn_x4
+MAX = mybir.AluOpType.max
+COPY = mybir.ActivationFunctionType.Copy
+
+P = 128
+PACK = 4
+HALF = 128
+HALVES = J // HALF
+N_TILES = N // P
+
+
+def load_words(queue, tile, words):
+    queue.dma_start(out=tile[:].bitcast(I32), in_=words.bitcast(I32))
+
+
+def load_scales(queue, stage, scales):
+    rows = scales[0].bitcast(I32).rearrange("(u q r) n -> q r u n", u=2, q=2)
+    for q in range(2):
+        queue.dma_start(out=stage[32 * q : 32 * q + 4], in_=rows[q])
+
+
+def load_plane(queues, plane, scales):
+    for q in range(4):
+        queues[q].dma_start(out=plane[32 * q : 32 * q + 4, :].bitcast(I32), in_=scales[0, 4 * q : 4 * q + 4, :].bitcast(I32))
+
+
+def lift_scales(nc, stage):
+    nc.vector.tensor_copy(out=stage[64:128, 0, :], in_=stage[0:64, 1, :])
+
+
+def tile_list_oneforboth_direct_skip_bestoftwo_kernel(
+    tc, xt_words, xt_scales, xo_words, xo_scales, w_words, w_scales, wb_words, wb_scales,
+    sx_words, sx_scales, ws_words, ws_scales, offs, offs2, offs3, offs4, out,
+):
+    nc = tc.nc
+    with ExitStack() as ctx:
+        lists = ctx.enter_context(tc.tile_pool(name="lists", bufs=1))
+        keep = ctx.enter_context(tc.tile_pool(name="keep", bufs=1))
+        psum = ctx.enter_context(tc.psum_pool(name="psum", bufs=1))
+
+        def sb(shape, dtype, name):
+            return keep.tile(shape, dtype, name=name, align_bytes=64)
+
+        o1 = lists.tile([P, J // 16], U16, name="o1")
+        o2 = lists.tile([P, J // 16], U16, name="o2")
+        o3 = lists.tile([P, E // 16], U16, name="o3")
+        o4 = lists.tile([P, E // 16], U16, name="o4")
+
+        xt_w = sb([P, T], U32, "xt_w")
+        xo_w = sb([P, Z], U32, "xo_w")
+        xt_s = sb([P, T], U8, "xt_s")
+        xo_s = sb([P, Z], U8, "xo_s")
+        w_w = sb([P, R], U16, "w_w")
+        w_st = sb([4, 4, R // 4], I32, "w_st")
+        w_pl = sb([P, R // 4], I32, "w_pl")
+        late_st = sb([P, 2, 3 * N // 4], I32, "late_st")
+        sx_w = sb([P, J], U32, "sx_w")
+        ws_w = sb([P, 2 * N], U8, "ws_w")
+        wb_w = sb([P, 2 * N], U8, "wb_w")
+
+        nc.gpsimd.memset(xt_s[:].bitcast(I32), 0)
+        nc.vector.memset(xo_s[:].bitcast(I32), 0)
+        nc.vector.memset(w_pl[:], 0)
+        nc.vector.memset(late_st[:], 0)
+
+        nc.sync.dma_start(out=w_st[:], in_=w_scales[0].bitcast(I32).rearrange("(q r) n -> r q n", q=4))
+        load_words(nc.sync, w_w, w_words[0])
+        nc.sync.dma_start(o1[:], offs)
+        load_words(nc.sync, xt_w, xt_words[0].rearrange("p c r -> p (c r)"))
+        load_plane((nc.sync, nc.scalar, nc.sync, nc.scalar), xt_s, xt_scales)
+        load_words(nc.sync, xo_w, xo_words[0].rearrange("p c r -> p (c r)"))
+        nc.sync.dma_start(o2[:], offs2)
+        load_plane((nc.sync,) * 4, xo_s, xo_scales)
+        load_words(nc.sync, sx_w, sx_words[0].rearrange("p c r -> p (c r)"))
+        load_words(nc.gpsimd, ws_w, ws_words[0])
+        load_words(nc.sync, wb_w, wb_words[0])
+        for i, scales in enumerate((ws_scales, sx_scales, wb_scales)):
+            load_scales(nc.sync, late_st[:, :, 64 * i : 64 * (i + 1)], scales)
+        nc.sync.dma_start(o3[:], offs3)
+        nc.sync.dma_start(o4[:], offs4)
+        w_s = w_pl[:].bitcast(U8)
+        late_s = late_st[:, 0, :].bitcast(U8)
+        ws_s, sx_s, wb_s = late_s[:, 0:N], late_s[:, N : 2 * N], late_s[:, 2 * N : 3 * N]
+
+        gt_s = sb([P, J], U8, "gt_s")
+        gt_w = [sb([P, HALF], U32, "gt_w%d" % h) for h in range(HALVES)]
+        go_s = sb([P, J], U8, "go_s")
+        go_w = [sb([P, HALF], U32, "go_w%d" % h) for h in range(HALVES)]
+        wd_w = sb([P, PACK, P], U16, "wd_w")
+        wd_s = sb([P, PACK, P], U8, "wd_s")
+
+        nc.scalar.copy(out=wd_w[:], in_=w_w[:].rearrange("p (m t) -> p t m", t=PACK))
+        for q in range(4):
+            nc.vector.tensor_copy(out=w_pl[32 * q : 32 * q + 4, :], in_=w_st[0:4, q, :])
+        nc.vector.tensor_copy(out=wd_s[:], in_=w_s.rearrange("p (m t) -> p t m", t=PACK))
+        nc.vector.tensor_copy(out=gt_s[:], in_=xt_s[:].indirect(o1[:]))
+        for h in range(HALVES):
+            nc.vector.tensor_copy(out=gt_w[h][:], in_=xt_w[:].indirect(o1[:, 8 * h : 8 * h + 8]))
+        nc.vector.tensor_copy(out=go_s[:], in_=xo_s[:].indirect(o2[:]))
+
+        def first_stage(bank, words, scales, fmt):
+            for t in range(PACK):
+                nc.tensor.matmul_mx(
+                    out=bank[:, t, :],
+                    lhsT=wd_w[:, t, :].bitcast(U8).bitcast(E2M1),
+                    lhsT_scale=wd_s[:, t, :],
+                    rhs=words.bitcast(fmt),
+                    rhs_scale=scales,
+                    start=True,
+                    stop=True,
+                )
+
+        cols = [slice(h * HALF, (h + 1) * HALF) for h in range(HALVES)]
+        a_sb = []
+        for h in range(HALVES):
+            a_ps = psum.tile([P, PACK, HALF], F32, name="a_ps%d" % h)
+            first_stage(a_ps, gt_w[h][:], gt_s[:, cols[h]], E5M2)
+            a_h = sb([P, HALF, PACK], F32, "a_sb%d" % h)
+            nc.scalar.activation(out=a_h[:], in_=a_ps[:].rearrange("p t j -> p j t"), func=COPY)
+            a_sb.append(a_h)
+
+        b_ps = []
+        for h in range(HALVES):
+            nc.vector.tensor_copy(out=go_w[h][:], in_=xo_w[:].indirect(o2[:, 8 * h : 8 * h + 8]))
+            b_h = psum.tile([P, PACK, HALF], F32, name="b_ps%d" % h)
+            first_stage(b_h, go_w[h][:], go_s[:, cols[h]], E4M3)
+            b_ps.append(b_h)
+
+        lift_scales(nc, late_st)
+        p_ps = {}
+        for h in range(HALVES):
+            for nt in range(N_TILES):
+                p_ps[nt, h] = psum.tile([P, HALF], F32, name="p_ps%d%d" % (nt, h))
+                nc.tensor.matmul_mx(
+                    out=p_ps[nt, h][:],
+                    lhsT=ws_w[:, 2 * P * nt : 2 * P * (nt + 1)].bitcast(E2M1),
+                    lhsT_scale=ws_s[:, P * nt : P * (nt + 1)],
+                    rhs=sx_w[:, cols[h]].bitcast(E4M3),
+                    rhs_scale=sx_s[:, cols[h]],
+                    start=True,
+                    stop=False,
+                )
+
+        hid = [sb([P, HALF, PACK], BF16, "hid%d" % h) for h in range(HALVES)]
+        hq_w = [sb([P, HALF], U32, "hq_w%d" % h) for h in range(HALVES)]
+        hq_s = [sb([P, HALF], U8, "hq_s%d" % h) for h in range(HALVES)]
+        for h in range(HALVES):
+            nc.vector.tensor_tensor(out=hid[h][:], in0=b_ps[h][:].rearrange("p t j -> p j t"), in1=a_sb[h][:], op=MAX)
+        p_sb = [sb([P, J], F32, "p_sb%d" % nt) for nt in range(N_TILES)]
+        for h in range(HALVES):
+            nc.vector.quantize_mx(
+                out=hq_w[h][:].bitcast(E4M3), scales=hq_s[h][:], in_=hid[h][:].rearrange("p j t -> p (j t)")
+            )
+            for nt in range(N_TILES):
+                nc.tensor.matmul_mx(
+                    out=p_ps[nt, h][:],
+                    lhsT=wb_w[:, 2 * P * nt : 2 * P * (nt + 1)].bitcast(E2M1),
+                    lhsT_scale=wb_s[:, P * nt : P * (nt + 1)],
+                    rhs=hq_w[h][:].bitcast(E4M3),
+                    rhs_scale=hq_s[h][:],
+                    start=False,
+                    stop=True,
+                )
+        nc.scalar.activation(out=p_sb[0][:, cols[0]], in_=p_ps[0, 0][:], func=COPY)
+        nc.scalar.activation(out=p_sb[1][:, cols[0]], in_=p_ps[1, 0][:], func=COPY)
+        nc.scalar.activation(out=p_sb[0][:, cols[1]], in_=p_ps[0, 1][:], func=COPY)
+        nc.vector.tensor_copy(out=p_sb[1][:, cols[1]], in_=p_ps[1, 1][:])
+
+        g3 = [sb([P, E], F32, "g3_%d" % nt) for nt in range(N_TILES)]
+        g4 = [sb([P, E], F32, "g4_%d" % nt) for nt in range(N_TILES)]
+        nc.scalar.activation(out=g3[0][:], in_=p_sb[0][:].indirect(o3[:]), func=COPY)
+        nc.scalar.activation(out=g4[0][:], in_=p_sb[0][:].indirect(o4[:]), func=COPY)
+        nc.vector.tensor_copy(out=g3[1][:], in_=p_sb[1][:].indirect(o3[:]))
+        nc.vector.tensor_copy(out=g4[1][:], in_=p_sb[1][:].indirect(o4[:]))
+        for nt, queue in ((1, nc.sync), (0, nc.scalar)):
+            y = sb([P, E], F32, "y%d" % nt)
+            nc.vector.tensor_tensor(out=y[:], in0=g3[nt][:], in1=g4[nt][:], op=MAX)
+            queue.dma_start(out=out[P * nt : P * (nt + 1), :], in_=y[:])

@@ -28,19 +28,18 @@ def load_words(queue, tile, words):
     queue.dma_start(out=tile[:].bitcast(I32), in_=words.bitcast(I32))
 
 
-def load_scales(queue, stage, scales):
-    rows = scales[0].bitcast(I32).rearrange("(u q r) n -> q r u n", u=2, q=2)
-    for q in range(2):
-        queue.dma_start(out=stage[32 * q : 32 * q + 4], in_=rows[q])
+def stage_scales(queue, stage, scales):
+    queue.dma_start(out=stage, in_=scales[0].bitcast(I32).rearrange("(q r) n -> r q n", q=4))
+
+
+def spread_scales(nc, plane, stage):
+    for q in range(4):
+        nc.vector.tensor_copy(out=plane[32 * q : 32 * q + 4, :], in_=stage[0:4, q, :])
 
 
 def load_plane(queues, plane, scales):
     for q in range(4):
         queues[q].dma_start(out=plane[32 * q : 32 * q + 4, :].bitcast(I32), in_=scales[0, 4 * q : 4 * q + 4, :].bitcast(I32))
-
-
-def lift_scales(nc, stage):
-    nc.vector.tensor_copy(out=stage[64:128, 0, :], in_=stage[0:64, 1, :])
 
 
 def tile_list_oneforboth_direct_skip_bestoftwo_kernel(
@@ -64,54 +63,49 @@ def tile_list_oneforboth_direct_skip_bestoftwo_kernel(
         xt_w = sb([P, T], U32, "xt_w")
         xo_w = sb([P, Z], U32, "xo_w")
         xt_s = sb([P, T], U8, "xt_s")
-        xo_s = sb([P, Z], U8, "xo_s")
+        xo_s = keep.tile([P, Z], U8, name="xo_s", tag="xo_s", align_bytes=64)
         w_w = sb([P, R], U16, "w_w")
         w_st = sb([4, 4, R // 4], I32, "w_st")
         w_pl = sb([P, R // 4], I32, "w_pl")
-        late_st = sb([P, 2, 3 * N // 4], I32, "late_st")
+        late_st = sb([4, 4, 3 * N // 4], I32, "late_st")
         sx_w = sb([P, J], U32, "sx_w")
         ws_w = sb([P, 2 * N], U8, "ws_w")
         wb_w = sb([P, 2 * N], U8, "wb_w")
 
-        nc.gpsimd.memset(xt_s[:].bitcast(I32), 0)
+        nc.vector.memset(xt_s[:].bitcast(I32), 0)
         nc.vector.memset(xo_s[:].bitcast(I32), 0)
         nc.vector.memset(w_pl[:], 0)
-        nc.vector.memset(late_st[:], 0)
 
-        nc.sync.dma_start(out=w_st[:], in_=w_scales[0].bitcast(I32).rearrange("(q r) n -> r q n", q=4))
-        load_words(nc.sync, w_w, w_words[0])
         nc.sync.dma_start(o1[:], offs)
-        load_words(nc.sync, xt_w, xt_words[0].rearrange("p c r -> p (c r)"))
+        stage_scales(nc.sync, w_st[:], w_scales)
+        load_words(nc.sync, w_w, w_words[0])
         load_plane((nc.sync, nc.scalar, nc.sync, nc.scalar), xt_s, xt_scales)
+        load_words(nc.sync, xt_w, xt_words[0].rearrange("p c r -> p (c r)"))
         load_words(nc.sync, xo_w, xo_words[0].rearrange("p c r -> p (c r)"))
         nc.sync.dma_start(o2[:], offs2)
         load_plane((nc.sync,) * 4, xo_s, xo_scales)
         load_words(nc.sync, sx_w, sx_words[0].rearrange("p c r -> p (c r)"))
-        load_words(nc.gpsimd, ws_w, ws_words[0])
+        load_words(nc.sync, ws_w, ws_words[0])
         load_words(nc.sync, wb_w, wb_words[0])
         for i, scales in enumerate((ws_scales, sx_scales, wb_scales)):
-            load_scales(nc.sync, late_st[:, :, 64 * i : 64 * (i + 1)], scales)
+            stage_scales(nc.gpsimd, late_st[:, :, 64 * i : 64 * (i + 1)], scales)
         nc.sync.dma_start(o3[:], offs3)
         nc.sync.dma_start(o4[:], offs4)
         w_s = w_pl[:].bitcast(U8)
-        late_s = late_st[:, 0, :].bitcast(U8)
-        ws_s, sx_s, wb_s = late_s[:, 0:N], late_s[:, N : 2 * N], late_s[:, 2 * N : 3 * N]
 
         gt_s = sb([P, J], U8, "gt_s")
         gt_w = [sb([P, HALF], U32, "gt_w%d" % h) for h in range(HALVES)]
-        go_s = sb([P, J], U8, "go_s")
+        go_s = [sb([P, HALF], U8, "go_s%d" % h) for h in range(HALVES)]
         go_w = [sb([P, HALF], U32, "go_w%d" % h) for h in range(HALVES)]
         wd_w = sb([P, PACK, P], U16, "wd_w")
         wd_s = sb([P, PACK, P], U8, "wd_s")
 
-        nc.scalar.copy(out=wd_w[:], in_=w_w[:].rearrange("p (m t) -> p t m", t=PACK))
-        for q in range(4):
-            nc.vector.tensor_copy(out=w_pl[32 * q : 32 * q + 4, :], in_=w_st[0:4, q, :])
-        nc.vector.tensor_copy(out=wd_s[:], in_=w_s.rearrange("p (m t) -> p t m", t=PACK))
+        spread_scales(nc, w_pl, w_st)
+        nc.vector.tensor_copy(out=wd_w[:], in_=w_w[:].rearrange("p (m t) -> p t m", t=PACK))
         nc.vector.tensor_copy(out=gt_s[:], in_=xt_s[:].indirect(o1[:]))
+        nc.vector.tensor_copy(out=wd_s[:], in_=w_s.rearrange("p (m t) -> p t m", t=PACK))
         for h in range(HALVES):
             nc.vector.tensor_copy(out=gt_w[h][:], in_=xt_w[:].indirect(o1[:, 8 * h : 8 * h + 8]))
-        nc.vector.tensor_copy(out=go_s[:], in_=xo_s[:].indirect(o2[:]))
 
         def first_stage(bank, words, scales, fmt):
             for t in range(PACK):
@@ -137,11 +131,15 @@ def tile_list_oneforboth_direct_skip_bestoftwo_kernel(
         b_ps = []
         for h in range(HALVES):
             nc.vector.tensor_copy(out=go_w[h][:], in_=xo_w[:].indirect(o2[:, 8 * h : 8 * h + 8]))
+            nc.vector.tensor_copy(out=go_s[h][:], in_=xo_s[:].indirect(o2[:, 8 * h : 8 * h + 8]))
             b_h = psum.tile([P, PACK, HALF], F32, name="b_ps%d" % h)
-            first_stage(b_h, go_w[h][:], go_s[:, cols[h]], E4M3)
+            first_stage(b_h, go_w[h][:], go_s[h][:], E4M3)
             b_ps.append(b_h)
 
-        lift_scales(nc, late_st)
+        late_pl = keep.tile([P, 3 * N // 4], I32, name="late_pl", tag="xo_s", align_bytes=64)
+        spread_scales(nc, late_pl, late_st)
+        late_s = late_pl[:].bitcast(U8)
+        ws_s, sx_s, wb_s = late_s[:, 0:N], late_s[:, N : 2 * N], late_s[:, 2 * N : 3 * N]
         p_ps = {}
         for h in range(HALVES):
             for nt in range(N_TILES):
@@ -166,7 +164,7 @@ def tile_list_oneforboth_direct_skip_bestoftwo_kernel(
             nc.vector.quantize_mx(
                 out=hq_w[h][:].bitcast(E4M3), scales=hq_s[h][:], in_=hid[h][:].rearrange("p j t -> p (j t)")
             )
-            for nt in range(N_TILES):
+            for nt in reversed(range(N_TILES)):
                 nc.tensor.matmul_mx(
                     out=p_ps[nt, h][:],
                     lhsT=wb_w[:, 2 * P * nt : 2 * P * (nt + 1)].bitcast(E2M1),
@@ -176,8 +174,8 @@ def tile_list_oneforboth_direct_skip_bestoftwo_kernel(
                     start=False,
                     stop=True,
                 )
-        nc.scalar.activation(out=p_sb[0][:, cols[0]], in_=p_ps[0, 0][:], func=COPY)
         nc.scalar.activation(out=p_sb[1][:, cols[0]], in_=p_ps[1, 0][:], func=COPY)
+        nc.scalar.activation(out=p_sb[0][:, cols[0]], in_=p_ps[0, 0][:], func=COPY)
         nc.scalar.activation(out=p_sb[0][:, cols[1]], in_=p_ps[0, 1][:], func=COPY)
         nc.vector.tensor_copy(out=p_sb[1][:, cols[1]], in_=p_ps[1, 1][:])
 
@@ -187,7 +185,7 @@ def tile_list_oneforboth_direct_skip_bestoftwo_kernel(
         nc.scalar.activation(out=g4[0][:], in_=p_sb[0][:].indirect(o4[:]), func=COPY)
         nc.vector.tensor_copy(out=g3[1][:], in_=p_sb[1][:].indirect(o3[:]))
         nc.vector.tensor_copy(out=g4[1][:], in_=p_sb[1][:].indirect(o4[:]))
-        for nt, queue in ((1, nc.sync), (0, nc.scalar)):
+        for nt, queue in ((0, nc.scalar), (1, nc.sync)):
             y = sb([P, E], F32, "y%d" % nt)
             nc.vector.tensor_tensor(out=y[:], in0=g3[nt][:], in1=g4[nt][:], op=MAX)
             queue.dma_start(out=out[P * nt : P * (nt + 1), :], in_=y[:])

@@ -67,7 +67,8 @@ def tile_list_oneforboth_direct_skip_bestoftwo_kernel(
         w_w = sb([P, R], U16, "w_w")
         w_st = sb([4, 4, R // 4], I32, "w_st")
         w_pl = sb([P, R // 4], I32, "w_pl")
-        late_st = sb([4, 4, 3 * N // 4], I32, "late_st")
+        late_st = keep.tile([4, 4, 2 * N // 4], I32, name="late_st", tag="late_st", align_bytes=64)
+        wb_s = sb([P, N], U8, "wb_s")
         sx_w = sb([P, J], U32, "sx_w")
         ws_w = sb([P, 2 * N], U8, "ws_w")
         wb_w = sb([P, 2 * N], U8, "wb_w")
@@ -75,6 +76,7 @@ def tile_list_oneforboth_direct_skip_bestoftwo_kernel(
         nc.vector.memset(xt_s[:].bitcast(I32), 0)
         nc.vector.memset(xo_s[:].bitcast(I32), 0)
         nc.vector.memset(w_pl[:], 0)
+        nc.vector.memset(wb_s[:].bitcast(I32), 0)
 
         nc.sync.dma_start(o1[:], offs)
         stage_scales(nc.sync, w_st[:], w_scales)
@@ -84,11 +86,12 @@ def tile_list_oneforboth_direct_skip_bestoftwo_kernel(
         load_words(nc.sync, xo_w, xo_words[0].rearrange("p c r -> p (c r)"))
         nc.sync.dma_start(o2[:], offs2)
         load_plane((nc.sync,) * 4, xo_s, xo_scales)
+        for i, scales in enumerate((ws_scales, sx_scales)):
+            stage_scales(nc.sync, late_st[:, :, 64 * i : 64 * (i + 1)], scales)
         load_words(nc.sync, sx_w, sx_words[0].rearrange("p c r -> p (c r)"))
         load_words(nc.sync, ws_w, ws_words[0])
+        load_plane((nc.sync,) * 4, wb_s, wb_scales)
         load_words(nc.sync, wb_w, wb_words[0])
-        for i, scales in enumerate((ws_scales, sx_scales, wb_scales)):
-            stage_scales(nc.gpsimd, late_st[:, :, 64 * i : 64 * (i + 1)], scales)
         nc.sync.dma_start(o3[:], offs3)
         nc.sync.dma_start(o4[:], offs4)
         w_s = w_pl[:].bitcast(U8)
@@ -136,10 +139,10 @@ def tile_list_oneforboth_direct_skip_bestoftwo_kernel(
             first_stage(b_h, go_w[h][:], go_s[h][:], E4M3)
             b_ps.append(b_h)
 
-        late_pl = keep.tile([P, 3 * N // 4], I32, name="late_pl", tag="xo_s", align_bytes=64)
+        late_pl = keep.tile([P, 2 * N // 4], I32, name="late_pl", tag="xo_s", align_bytes=64)
         spread_scales(nc, late_pl, late_st)
         late_s = late_pl[:].bitcast(U8)
-        ws_s, sx_s, wb_s = late_s[:, 0:N], late_s[:, N : 2 * N], late_s[:, 2 * N : 3 * N]
+        ws_s, sx_s = late_s[:, 0:N], late_s[:, N : 2 * N]
         p_ps = {}
         for h in range(HALVES):
             for nt in range(N_TILES):
@@ -154,15 +157,15 @@ def tile_list_oneforboth_direct_skip_bestoftwo_kernel(
                     stop=False,
                 )
 
-        hid = [sb([P, HALF, PACK], BF16, "hid%d" % h) for h in range(HALVES)]
+        hid = keep.tile([P, HALVES, HALF, PACK], BF16, name="hid", tag="late_st", align_bytes=64)
         hq_w = [sb([P, HALF], U32, "hq_w%d" % h) for h in range(HALVES)]
         hq_s = [sb([P, HALF], U8, "hq_s%d" % h) for h in range(HALVES)]
         for h in range(HALVES):
-            nc.vector.tensor_tensor(out=hid[h][:], in0=b_ps[h][:].rearrange("p t j -> p j t"), in1=a_sb[h][:], op=MAX)
+            nc.vector.tensor_tensor(out=hid[:, h], in0=b_ps[h][:].rearrange("p t j -> p j t"), in1=a_sb[h][:], op=MAX)
         p_sb = [sb([P, J], F32, "p_sb%d" % nt) for nt in range(N_TILES)]
         for h in range(HALVES):
             nc.vector.quantize_mx(
-                out=hq_w[h][:].bitcast(E4M3), scales=hq_s[h][:], in_=hid[h][:].rearrange("p j t -> p (j t)")
+                out=hq_w[h][:].bitcast(E4M3), scales=hq_s[h][:], in_=hid[:, h].rearrange("p j t -> p (j t)")
             )
             for nt in reversed(range(N_TILES)):
                 nc.tensor.matmul_mx(

@@ -104,7 +104,7 @@ def tile_list_oneforboth_direct_skip_bestoftwo_kernel(
         wd_s = sb([P, PACK, P], U8, "wd_s")
 
         spread_scales(nc, w_pl, w_st)
-        nc.vector.tensor_copy(out=wd_w[:], in_=w_w[:].rearrange("p (m t) -> p t m", t=PACK))
+        nc.scalar.copy(out=wd_w[:], in_=w_w[:].rearrange("p (m t) -> p t m", t=PACK))
         nc.vector.tensor_copy(out=gt_s[:], in_=xt_s[:].indirect(o1[:]))
         nc.vector.tensor_copy(out=wd_s[:], in_=w_s.rearrange("p (m t) -> p t m", t=PACK))
         for h in range(HALVES):
@@ -179,8 +179,8 @@ def tile_list_oneforboth_direct_skip_bestoftwo_kernel(
                 )
         nc.scalar.activation(out=p_sb[1][:, cols[0]], in_=p_ps[1, 0][:], func=COPY)
         nc.scalar.activation(out=p_sb[0][:, cols[0]], in_=p_ps[0, 0][:], func=COPY)
-        nc.scalar.activation(out=p_sb[0][:, cols[1]], in_=p_ps[0, 1][:], func=COPY)
-        nc.vector.tensor_copy(out=p_sb[1][:, cols[1]], in_=p_ps[1, 1][:])
+        nc.scalar.activation(out=p_sb[1][:, cols[1]], in_=p_ps[1, 1][:], func=COPY)
+        nc.vector.tensor_copy(out=p_sb[0][:, cols[1]], in_=p_ps[0, 1][:])
 
         g3 = [sb([P, E], F32, "g3_%d" % nt) for nt in range(N_TILES)]
         g4 = [sb([P, E], F32, "g4_%d" % nt) for nt in range(N_TILES)]

from contextlib import ExitStack

import concourse.mybir as mybir

K, T, Z, J, R, N, L, E = 512, 1024, 1024, 256, 512, 256, 512, 128
FLOPS = 2 * (2 * K * R * J + R * N * J + L * N * J)

F32 = mybir.dt.float32
BF16 = mybir.dt.bfloat16
I32 = mybir.dt.int32
U32 = mybir.dt.uint32
U16 = mybir.dt.uint16
U8 = mybir.dt.uint8
E4M3 = mybir.dt.float8_e4m3fn_x4
E5M2 = mybir.dt.float8_e5m2_x4
E2M1 = mybir.dt.float4_e2m1fn_x4
MAX = mybir.AluOpType.max
COPY = mybir.ActivationFunctionType.Copy

P = 128
PACK = 4
HALF = 128
HALVES = J // HALF
N_TILES = N // P


def load_words(queue, tile, words):
    queue.dma_start(out=tile[:].bitcast(I32), in_=words.bitcast(I32))


def stage_scales(queue, stage, scales):
    queue.dma_start(out=stage, in_=scales[0].bitcast(I32).rearrange("(q r) n -> r q n", q=4))


def spread_scales(nc, plane, stage):
    for q in range(4):
        nc.vector.tensor_copy(out=plane[32 * q : 32 * q + 4, :], in_=stage[0:4, q, :])


def load_plane(queues, plane, scales):
    for q in range(4):
        queues[q].dma_start(out=plane[32 * q : 32 * q + 4, :].bitcast(I32), in_=scales[0, 4 * q : 4 * q + 4, :].bitcast(I32))


def tile_list_oneforboth_direct_skip_bestoftwo_kernel(
    tc, xt_words, xt_scales, xo_words, xo_scales, w_words, w_scales, wb_words, wb_scales,
    sx_words, sx_scales, ws_words, ws_scales, offs, offs2, offs3, offs4, out,
):
    nc = tc.nc
    with ExitStack() as ctx:
        lists = ctx.enter_context(tc.tile_pool(name="lists", bufs=1))
        keep = ctx.enter_context(tc.tile_pool(name="keep", bufs=1))
        psum = ctx.enter_context(tc.psum_pool(name="psum", bufs=1))

        def sb(shape, dtype, name):
            return keep.tile(shape, dtype, name=name, align_bytes=64)

        o1 = lists.tile([P, J // 16], U16, name="o1")
        o2 = lists.tile([P, J // 16], U16, name="o2")
        o3 = lists.tile([P, E // 16], U16, name="o3")
        o4 = lists.tile([P, E // 16], U16, name="o4")

        xt_w = sb([P, T], U32, "xt_w")
        xo_w = sb([P, Z], U32, "xo_w")
        xt_s = sb([P, T], U8, "xt_s")
        xo_s = keep.tile([P, Z], U8, name="xo_s", tag="xo_s", align_bytes=64)
        w_w = sb([P, R], U16, "w_w")
        w_st = sb([4, 4, R // 4], I32, "w_st")
        w_pl = sb([P, R // 4], I32, "w_pl")
        late_st = keep.tile([4, 4, 2 * N // 4], I32, name="late_st", tag="late_st", align_bytes=64)
        wb_s = sb([P, N], U8, "wb_s")
        sx_w = sb([P, J], U32, "sx_w")
        ws_w = sb([P, 2 * N], U8, "ws_w")
        wb_w = sb([P, 2 * N], U8, "wb_w")

        nc.vector.memset(xt_s[:].bitcast(I32), 0)
        nc.vector.memset(xo_s[:].bitcast(I32), 0)
        nc.vector.memset(w_pl[:], 0)
        nc.vector.memset(wb_s[:].bitcast(I32), 0)

        nc.sync.dma_start(o1[:], offs)
        stage_scales(nc.sync, w_st[:], w_scales)
        load_words(nc.sync, w_w, w_words[0])
        load_plane((nc.sync, nc.scalar, nc.sync, nc.scalar), xt_s, xt_scales)
        load_words(nc.sync, xt_w, xt_words[0].rearrange("p c r -> p (c r)"))
        load_words(nc.sync, xo_w, xo_words[0].rearrange("p c r -> p (c r)"))
        nc.sync.dma_start(o2[:], offs2)
        load_plane((nc.sync,) * 4, xo_s, xo_scales)
        for i, scales in enumerate((ws_scales, sx_scales)):
            stage_scales(nc.sync, late_st[:, :, 64 * i : 64 * (i + 1)], scales)
        load_words(nc.sync, sx_w, sx_words[0].rearrange("p c r -> p (c r)"))
        load_words(nc.sync, ws_w, ws_words[0])
        load_plane((nc.sync,) * 4, wb_s, wb_scales)
        load_words(nc.sync, wb_w, wb_words[0])
        nc.sync.dma_start(o3[:], offs3)
        nc.sync.dma_start(o4[:], offs4)
        w_s = w_pl[:].bitcast(U8)

        gt_s = sb([P, J], U8, "gt_s")
        gt_w = [sb([P, HALF], U32, "gt_w%d" % h) for h in range(HALVES)]
        go_s = [sb([P, HALF], U8, "go_s%d" % h) for h in range(HALVES)]
        go_w = [sb([P, HALF], U32, "go_w%d" % h) for h in range(HALVES)]
        wd_w = sb([P, PACK, P], U16, "wd_w")
        wd_s = sb([P, PACK, P], U8, "wd_s")

        spread_scales(nc, w_pl, w_st)
        nc.scalar.copy(out=wd_w[:], in_=w_w[:].rearrange("p (m t) -> p t m", t=PACK))
        nc.vector.tensor_copy(out=gt_s[:], in_=xt_s[:].indirect(o1[:]))
        nc.vector.tensor_copy(out=wd_s[:], in_=w_s.rearrange("p (m t) -> p t m", t=PACK))
        for h in range(HALVES):
            nc.vector.tensor_copy(out=gt_w[h][:], in_=xt_w[:].indirect(o1[:, 8 * h : 8 * h + 8]))

        def first_stage(bank, words, scales, fmt):
            for t in range(PACK):
                nc.tensor.matmul_mx(
                    out=bank[:, t, :],
                    lhsT=wd_w[:, t, :].bitcast(U8).bitcast(E2M1),
                    lhsT_scale=wd_s[:, t, :],
                    rhs=words.bitcast(fmt),
                    rhs_scale=scales,
                    start=True,
                    stop=True,
                )

        cols = [slice(h * HALF, (h + 1) * HALF) for h in range(HALVES)]
        a_sb = []
        for h in range(HALVES):
            a_ps = psum.tile([P, PACK, HALF], F32, name="a_ps%d" % h)
            first_stage(a_ps, gt_w[h][:], gt_s[:, cols[h]], E5M2)
            a_h = sb([P, HALF, PACK], F32, "a_sb%d" % h)
            nc.scalar.activation(out=a_h[:], in_=a_ps[:].rearrange("p t j -> p j t"), func=COPY)
            a_sb.append(a_h)

        b_ps = []
        for h in range(HALVES):
            nc.vector.tensor_copy(out=go_w[h][:], in_=xo_w[:].indirect(o2[:, 8 * h : 8 * h + 8]))
            nc.vector.tensor_copy(out=go_s[h][:], in_=xo_s[:].indirect(o2[:, 8 * h : 8 * h + 8]))
            b_h = psum.tile([P, PACK, HALF], F32, name="b_ps%d" % h)
            first_stage(b_h, go_w[h][:], go_s[h][:], E4M3)
            b_ps.append(b_h)

        late_pl = keep.tile([P, 2 * N // 4], I32, name="late_pl", tag="xo_s", align_bytes=64)
        spread_scales(nc, late_pl, late_st)
        late_s = late_pl[:].bitcast(U8)
        ws_s, sx_s = late_s[:, 0:N], late_s[:, N : 2 * N]
        p_ps = {}
        for h in range(HALVES):
            for nt in range(N_TILES):
                p_ps[nt, h] = psum.tile([P, HALF], F32, name="p_ps%d%d" % (nt, h))
                nc.tensor.matmul_mx(
                    out=p_ps[nt, h][:],
                    lhsT=ws_w[:, 2 * P * nt : 2 * P * (nt + 1)].bitcast(E2M1),
                    lhsT_scale=ws_s[:, P * nt : P * (nt + 1)],
                    rhs=sx_w[:, cols[h]].bitcast(E4M3),
                    rhs_scale=sx_s[:, cols[h]],
                    start=True,
                    stop=False,
                )

        hid = keep.tile([P, HALVES, HALF, PACK], BF16, name="hid", tag="late_st", align_bytes=64)
        hq_w = [sb([P, HALF], U32, "hq_w%d" % h) for h in range(HALVES)]
        hq_s = [sb([P, HALF], U8, "hq_s%d" % h) for h in range(HALVES)]
        for h in range(HALVES):
            nc.vector.tensor_tensor(out=hid[:, h], in0=b_ps[h][:].rearrange("p t j -> p j t"), in1=a_sb[h][:], op=MAX)
        p_sb = [sb([P, J], F32, "p_sb%d" % nt) for nt in range(N_TILES)]
        for h in range(HALVES):
            nc.vector.quantize_mx(
                out=hq_w[h][:].bitcast(E4M3), scales=hq_s[h][:], in_=hid[:, h].rearrange("p j t -> p (j t)")
            )
            for nt in reversed(range(N_TILES)):
                nc.tensor.matmul_mx(
                    out=p_ps[nt, h][:],
                    lhsT=wb_w[:, 2 * P * nt : 2 * P * (nt + 1)].bitcast(E2M1),
                    lhsT_scale=wb_s[:, P * nt : P * (nt + 1)],
                    rhs=hq_w[h][:].bitcast(E4M3),
                    rhs_scale=hq_s[h][:],
                    start=False,
                    stop=True,
                )
        nc.scalar.activation(out=p_sb[1][:, cols[0]], in_=p_ps[1, 0][:], func=COPY)
        nc.scalar.activation(out=p_sb[0][:, cols[0]], in_=p_ps[0, 0][:], func=COPY)
        nc.scalar.activation(out=p_sb[1][:, cols[1]], in_=p_ps[1, 1][:], func=COPY)
        nc.vector.tensor_copy(out=p_sb[0][:, cols[1]], in_=p_ps[0, 1][:])

        g3 = [sb([P, E], F32, "g3_%d" % nt) for nt in range(N_TILES)]
        g4 = [sb([P, E], F32, "g4_%d" % nt) for nt in range(N_TILES)]
        nc.scalar.activation(out=g3[0][:], in_=p_sb[0][:].indirect(o3[:]), func=COPY)
        nc.scalar.activation(out=g4[0][:], in_=p_sb[0][:].indirect(o4[:]), func=COPY)
        nc.vector.tensor_copy(out=g3[1][:], in_=p_sb[1][:].indirect(o3[:]))
        nc.vector.tensor_copy(out=g4[1][:], in_=p_sb[1][:].indirect(o4[:]))
        for nt, queue in ((0, nc.scalar), (1, nc.sync)):
            y = sb([P, E], F32, "y%d" % nt)
            nc.vector.tensor_tensor(out=y[:], in0=g3[nt][:], in1=g4[nt][:], op=MAX)
            queue.dma_start(out=out[P * nt : P * (nt + 1), :], in_=y[:])
